import numpy as np
import ml_dtypes

BF16 = ml_dtypes.bfloat16


def bf(x):
    return np.asarray(x, np.float32).astype(BF16)


def f32(x):
    return np.asarray(x, np.float32)


def f64(x):
    return np.asarray(x).astype(np.float64)


def striped(idx):
    return np.tile(idx.reshape(-1, 16).T, (8, 1))


S, K, M, N, V, D = 1024, 128, 256, 512, 32, 16


def setup_inputs():
    return {"table": bf(np.random.standard_normal((K, S))), "w": bf(np.random.standard_normal((K, M)) / np.sqrt(K)), "x": bf(np.random.standard_normal((K, V))), "wc": bf(np.random.standard_normal((K, M)) / np.sqrt(K)), "b": f32(0.5 * np.random.standard_normal((M, 1))), "offs": striped(np.random.permutation(S)[:N])}


def reference(table, w, x, wc, b, offs):
    idx = offs[:16].T.reshape(-1)
    y = (f64(w).T @ f64(table)[:, idx]).reshape(M, V, D)
    u = f64(wc).T @ f64(x) + f64(b)
    z = y + u[:, :, None]
    z = np.maximum(z, 0.0)
    return z.max(axis=2)

@@ -1,0 +1,68 @@
+import concourse.mybir as mybir
+
+P = 128
+NEIGHBOURS = 16
+
+FLOPS = 2 * 128 * 256 * (512 + 32)
+
+BF16, F32, U16 = mybir.dt.bfloat16, mybir.dt.float32, mybir.dt.uint16
+ADD, MAX = mybir.AluOpType.add, mybir.AluOpType.max
+
+
+def tile_rows_ecv_sub_relu_kernel(tc, table, w, x, wc, b, offs, out):
+    nc = tc.nc
+    points = table.shape[1]
+    features_out = w.shape[1]
+    centres = x.shape[1]
+    blocks = features_out // P
+
+    with (
+        tc.tile_pool(name="held", bufs=1) as held,
+        tc.psum_pool(name="psum", bufs=1) as psum,
+    ):
+        table_sb = held.tile([P, points], BF16)
+        w_sb = held.tile([P, features_out], BF16)
+        wc_sb = held.tile([P, features_out], BF16)
+        x_sb = held.tile([P, centres], BF16)
+        bias = held.tile([P, blocks], F32)
+        offsets = held.tile(list(offs.shape), U16)
+
+        nc.sync.dma_start(table_sb[:], table)
+        nc.scalar.dma_start(w_sb[:], w)
+        nc.sync.dma_start(offsets[:], offs)
+        nc.sync.dma_start(wc_sb[:], wc)
+        nc.sync.dma_start(x_sb[:], x)
+        nc.sync.dma_start(bias[:], b.rearrange("(a p) o -> p (a o)", p=P))
+
+        neighbour_banks = []
+        for a in range(blocks):
+            bank = psum.tile([P, centres * NEIGHBOURS], F32, name=f"neighbours{a}")
+            nc.tensor.matmul(
+                bank[:],
+                w_sb[:, a * P : (a + 1) * P],
+                table_sb[:].indirect(offsets[:]),
+                start=True,
+                stop=True,
+            )
+            neighbour_banks.append(bank)
+
+        result = held.tile([P, blocks, centres], F32)
+        for a in range(blocks):
+            centre_bank = psum.tile([P, centres], F32, name=f"centres{a}")
+            nc.tensor.matmul(
+                centre_bank[:], wc_sb[:, a * P : (a + 1) * P], x_sb[:], start=True, stop=True
+            )
+            largest = held.tile([P, centres], F32, name=f"largest{a}")
+            nc.vector.tensor_reduce(
+                largest[:],
+                neighbour_banks[a][:].rearrange("p (v t) -> p v t", t=NEIGHBOURS),
+                mybir.AxisListType.X,
+                MAX,
+            )
+            summed = held.tile([P, centres], F32, name=f"summed{a}")
+            nc.vector.scalar_tensor_tensor(
+                summed[:], centre_bank[:], bias[:, a : a + 1], largest[:], ADD, ADD
+            )
+            nc.vector.tensor_scalar_max(result[:, a, :], summed[:], 0.0)
+
+        nc.sync.dma_start(out.rearrange("(a p) v -> p a v", p=P), result[:])

@@ -2,6 +2,8 @@ import concourse.mybir as mybir
 
 P = 128
 NEIGHBOURS = 16
+ENTRIES_PER_COLUMN = 16
+PIECES = 2
 
 FLOPS = 2 * 128 * 256 * (512 + 32)
 
@@ -15,6 +17,9 @@ def tile_rows_ecv_sub_relu_kernel(tc, table, w, x, wc, b, offs, out):
     features_out = w.shape[1]
     centres = x.shape[1]
     blocks = features_out // P
+    piece_centres = centres // PIECES
+    piece_entries = piece_centres * NEIGHBOURS
+    piece_columns = piece_entries // ENTRIES_PER_COLUMN
 
     with (
         tc.tile_pool(name="held", bufs=1) as held,
@@ -32,37 +37,39 @@ def tile_rows_ecv_sub_relu_kernel(tc, table, w, x, wc, b, offs, out):
         nc.sync.dma_start(offsets[:], offs)
         nc.sync.dma_start(wc_sb[:], wc)
         nc.sync.dma_start(x_sb[:], x)
-        nc.sync.dma_start(bias[:], b.rearrange("(a p) o -> p (a o)", p=P))
+        nc.sync.dma_start(bias[:], b.rearrange("(p a) o -> p (a o)", a=blocks))
 
-        neighbour_banks = []
+        w_blocks = w_sb[:].rearrange("k (p a) -> k a p", a=blocks)
+        wc_blocks = wc_sb[:].rearrange("k (p a) -> k a p", a=blocks)
+
+        largest = held.tile([P, blocks, centres], F32)
         for a in range(blocks):
-            bank = psum.tile([P, centres * NEIGHBOURS], F32, name=f"neighbours{a}")
-            nc.tensor.matmul(
-                bank[:],
-                w_sb[:, a * P : (a + 1) * P],
-                table_sb[:].indirect(offsets[:]),
-                start=True,
-                stop=True,
-            )
-            neighbour_banks.append(bank)
+            for piece in range(PIECES):
+                neighbour_bank = psum.tile([P, piece_entries], F32, name=f"neighbours{a}_{piece}")
+                nc.tensor.matmul(
+                    neighbour_bank[:],
+                    w_blocks[:, a, :],
+                    table_sb[:].indirect(
+                        offsets[:, piece * piece_columns : (piece + 1) * piece_columns]
+                    ),
+                    start=True,
+                    stop=True,
+                )
+                nc.vector.tensor_reduce(
+                    largest[:, a, piece * piece_centres : (piece + 1) * piece_centres],
+                    neighbour_bank[:].rearrange("p (v t) -> p v t", t=NEIGHBOURS),
+                    mybir.AxisListType.X,
+                    MAX,
+                )
 
-        result = held.tile([P, blocks, centres], F32)
+        summed = held.tile([P, blocks, centres], F32)
         for a in range(blocks):
             centre_bank = psum.tile([P, centres], F32, name=f"centres{a}")
-            nc.tensor.matmul(
-                centre_bank[:], wc_sb[:, a * P : (a + 1) * P], x_sb[:], start=True, stop=True
-            )
-            largest = held.tile([P, centres], F32, name=f"largest{a}")
-            nc.vector.tensor_reduce(
-                largest[:],
-                neighbour_banks[a][:].rearrange("p (v t) -> p v t", t=NEIGHBOURS),
-                mybir.AxisListType.X,
-                MAX,
-            )
-            summed = held.tile([P, centres], F32, name=f"summed{a}")
+            nc.tensor.matmul(centre_bank[:], wc_blocks[:, a, :], x_sb[:], start=True, stop=True)
             nc.vector.scalar_tensor_tensor(
-                summed[:], centre_bank[:], bias[:, a : a + 1], largest[:], ADD, ADD
+                summed[:, a, :], centre_bank[:], bias[:, a : a + 1], largest[:, a, :], ADD, ADD
             )
-            nc.vector.tensor_scalar_max(result[:, a, :], summed[:], 0.0)
 
-        nc.sync.dma_start(out.rearrange("(a p) v -> p a v", p=P), result[:])
+        result = held.tile([P, blocks, centres], F32)
+        nc.vector.tensor_scalar_max(result[:], summed[:], 0.0)
+        nc.sync.dma_start(out.rearrange("(p a) v -> p a v", a=blocks), result[:])

import concourse.mybir as mybir

P = 128
NEIGHBOURS = 16
ENTRIES_PER_COLUMN = 16
PIECES = 2

FLOPS = 2 * 128 * 256 * (512 + 32)

BF16, F32, U16 = mybir.dt.bfloat16, mybir.dt.float32, mybir.dt.uint16
ADD, MAX = mybir.AluOpType.add, mybir.AluOpType.max


def tile_rows_ecv_sub_relu_kernel(tc, table, w, x, wc, b, offs, out):
    nc = tc.nc
    points = table.shape[1]
    features_out = w.shape[1]
    centres = x.shape[1]
    blocks = features_out // P
    piece_centres = centres // PIECES
    piece_entries = piece_centres * NEIGHBOURS
    piece_columns = piece_entries // ENTRIES_PER_COLUMN

    with (
        tc.tile_pool(name="held", bufs=1) as held,
        tc.psum_pool(name="psum", bufs=1) as psum,
    ):
        table_sb = held.tile([P, points], BF16)
        w_sb = held.tile([P, features_out], BF16)
        wc_sb = held.tile([P, features_out], BF16)
        x_sb = held.tile([P, centres], BF16)
        bias = held.tile([P, blocks], F32)
        offsets = held.tile(list(offs.shape), U16)

        nc.sync.dma_start(table_sb[:], table)
        nc.scalar.dma_start(w_sb[:], w)
        nc.sync.dma_start(offsets[:], offs)
        nc.sync.dma_start(wc_sb[:], wc)
        nc.sync.dma_start(x_sb[:], x)
        nc.sync.dma_start(bias[:], b.rearrange("(p a) o -> p (a o)", a=blocks))

        w_blocks = w_sb[:].rearrange("k (p a) -> k a p", a=blocks)
        wc_blocks = wc_sb[:].rearrange("k (p a) -> k a p", a=blocks)

        largest = held.tile([P, blocks, centres], F32)
        for a in range(blocks):
            for piece in range(PIECES):
                neighbour_bank = psum.tile([P, piece_entries], F32, name=f"neighbours{a}_{piece}")
                nc.tensor.matmul(
                    neighbour_bank[:],
                    w_blocks[:, a, :],
                    table_sb[:].indirect(
                        offsets[:, piece * piece_columns : (piece + 1) * piece_columns]
                    ),
                    start=True,
                    stop=True,
                )
                nc.vector.tensor_reduce(
                    largest[:, a, piece * piece_centres : (piece + 1) * piece_centres],
                    neighbour_bank[:].rearrange("p (v t) -> p v t", t=NEIGHBOURS),
                    mybir.AxisListType.X,
                    MAX,
                )

        summed = held.tile([P, blocks, centres], F32)
        for a in range(blocks):
            centre_bank = psum.tile([P, centres], F32, name=f"centres{a}")
            nc.tensor.matmul(centre_bank[:], wc_blocks[:, a, :], x_sb[:], start=True, stop=True)
            nc.vector.scalar_tensor_tensor(
                summed[:, a, :], centre_bank[:], bias[:, a : a + 1], largest[:, a, :], ADD, ADD
            )

        result = held.tile([P, blocks, centres], F32)
        nc.vector.tensor_scalar_max(result[:], summed[:], 0.0)
        nc.sync.dma_start(out.rearrange("(p a) v -> p a v", a=blocks), result[:])
